import numpy as np
import ml_dtypes

BF16 = ml_dtypes.bfloat16


def bf(x):
    return np.asarray(x, np.float32).astype(BF16)


def f32(x):
    return np.asarray(x, np.float32)


def f64(x):
    return np.asarray(x).astype(np.float64)


def striped(idx):
    return np.tile(idx.reshape(-1, 16).T, (8, 1))


def rows(idx, k):
    return np.tile(idx, (k, 1))


def look(tab, idx):
    return np.take_along_axis(f64(tab), rows(idx, len(tab)), axis=1)


K, S, D, V, N, M = 128, 256, 1, 256, 256, 256


def setup_inputs():
    return {"tab": f32(0.7 * np.random.standard_normal((D, K, S))), "base": f32(np.random.standard_normal((K, V))), "w": bf(np.random.standard_normal((K, M)) / np.sqrt(K)), "b": f32(0.5 * np.random.standard_normal((M, 1))), "offs": striped(np.random.randint(0, S, N))}


def reference(tab, base, w, b, offs):
    idx = offs[:16].T.reshape(-1)
    x = f64(base) + sum(look(tab[d], idx[d * V:(d + 1) * V]) for d in range(D))
    y = f64(w).T @ x
    return np.maximum(y + f64(b), 0.0)

@@ -1,0 +1,46 @@
+import concourse.mybir as mybir
+
+K, S, N, M = 128, 256, 256, 256
+P = 128
+FLOPS = 2 * K * M * N + K * N
+F32, BF16, U16 = mybir.dt.float32, mybir.dt.bfloat16, mybir.dt.uint16
+ADD, MAX = mybir.AluOpType.add, mybir.AluOpType.max
+RELU = mybir.ActivationFunctionType.Relu
+
+
+def tile_lookup_res_add_relu_kernel(tc, tab, base, w, b, offs, out):
+    nc = tc.nc
+    with (
+        tc.tile_pool(name="held", bufs=1) as held,
+        tc.psum_pool(name="psum", bufs=1) as psum,
+    ):
+        offsets = held.tile([P, N // 16], U16, name="offsets")
+        codebook = held.tile([P, S], F32, name="codebook")
+        base_sb = held.tile([P, N], F32, name="base_sb")
+        weights = held.tile([P, M], BF16, name="weights")
+        biases = [held.tile([P, 1], F32, name=f"bias{c}") for c in range(M // P)]
+
+        nc.sync.dma_start(offsets[:], offs)
+        nc.sync.dma_start(codebook[:], tab[0])
+        nc.scalar.dma_start(base_sb[:], base)
+        nc.gpsimd.dma_start(weights[:], w)
+        for c in range(M // P):
+            nc.sync.dma_start(biases[c][:], b[c * P : (c + 1) * P, :])
+
+        x = held.tile([P, N], F32, name="x")
+        nc.vector.tensor_tensor(x[:], codebook[:].indirect(offsets[:]), base_sb[:], ADD)
+        x_bf = held.tile([P, N], BF16, name="x_bf")
+        nc.vector.tensor_copy(x_bf[:], x[:])
+
+        products = []
+        for c in range(M // P):
+            y = psum.tile([P, N], F32, name=f"y{c}")
+            nc.tensor.matmul(y[:], weights[:, c * P : (c + 1) * P], x_bf[:], start=True, stop=True)
+            products.append(y)
+
+        out0 = held.tile([P, N], F32, name="out0")
+        nc.scalar.activation(out0[:], products[0][:], RELU, bias=biases[0][:])
+        nc.scalar.dma_start(out[0:P, :], out0[:])
+        out1 = held.tile([P, N], F32, name="out1")
+        nc.vector.tensor_scalar(out1[:], products[1][:], biases[1][:], 0.0, ADD, MAX)
+        nc.sync.dma_start(out[P : 2 * P, :], out1[:])

@@ -2,6 +2,7 @@ import concourse.mybir as mybir
 
 K, S, N, M = 128, 256, 256, 256
 P = 128
+HALF = N // 2
 FLOPS = 2 * K * M * N + K * N
 F32, BF16, U16 = mybir.dt.float32, mybir.dt.bfloat16, mybir.dt.uint16
 ADD, MAX = mybir.AluOpType.add, mybir.AluOpType.max
@@ -23,24 +24,33 @@ def tile_lookup_res_add_relu_kernel(tc, tab, base, w, b, offs, out):
         nc.sync.dma_start(offsets[:], offs)
         nc.sync.dma_start(codebook[:], tab[0])
         nc.scalar.dma_start(base_sb[:], base)
-        nc.gpsimd.dma_start(weights[:], w)
+        nc.scalar.dma_start(weights[:], w)
         for c in range(M // P):
             nc.sync.dma_start(biases[c][:], b[c * P : (c + 1) * P, :])
 
-        x = held.tile([P, N], F32, name="x")
-        nc.vector.tensor_tensor(x[:], codebook[:].indirect(offsets[:]), base_sb[:], ADD)
-        x_bf = held.tile([P, N], BF16, name="x_bf")
-        nc.vector.tensor_copy(x_bf[:], x[:])
+        zeros = held.tile([P, 1], F32, name="zeros")
+        nc.vector.memset(zeros[:], 0.0)
+        warm = held.tile([P, 1], F32, name="warm")
+        nc.scalar.activation(warm[:], zeros[:], RELU)
 
-        products = []
-        for c in range(M // P):
-            y = psum.tile([P, N], F32, name=f"y{c}")
-            nc.tensor.matmul(y[:], weights[:, c * P : (c + 1) * P], x_bf[:], start=True, stop=True)
-            products.append(y)
+        x_bf = []
+        for h in range(2):
+            columns = slice(h * HALF, (h + 1) * HALF)
+            entries = offsets[:, h * HALF // 16 : (h + 1) * HALF // 16]
+            x = held.tile([P, HALF], F32, name=f"x{h}")
+            nc.vector.tensor_tensor(x[:], codebook[:].indirect(entries), base_sb[:, columns], ADD)
+            x_bf.append(held.tile([P, HALF], BF16, name=f"x_bf{h}"))
+            nc.vector.tensor_copy(x_bf[h][:], x[:])
 
         out0 = held.tile([P, N], F32, name="out0")
-        nc.scalar.activation(out0[:], products[0][:], RELU, bias=biases[0][:])
-        nc.scalar.dma_start(out[0:P, :], out0[:])
         out1 = held.tile([P, N], F32, name="out1")
-        nc.vector.tensor_scalar(out1[:], products[1][:], biases[1][:], 0.0, ADD, MAX)
-        nc.sync.dma_start(out[P : 2 * P, :], out1[:])
+        for h in range(2):
+            columns = slice(h * HALF, (h + 1) * HALF)
+            y0 = psum.tile([P, HALF], F32, name=f"y0_{h}")
+            nc.tensor.matmul(y0[:], weights[:, 0:P], x_bf[h][:], start=True, stop=True)
+            y1 = psum.tile([P, HALF], F32, name=f"y1_{h}")
+            nc.tensor.matmul(y1[:], weights[:, P : 2 * P], x_bf[h][:], start=True, stop=True)
+            nc.scalar.activation(out0[:, columns], y0[:], RELU, bias=biases[0][:])
+            nc.vector.tensor_scalar(out1[:, columns], y1[:], biases[1][:], 0.0, ADD, MAX)
+            nc.scalar.dma_start(out[0:P, columns], out0[:, columns])
+            nc.sync.dma_start(out[P : 2 * P, columns], out1[:, columns])

@@ -19,14 +19,14 @@ def tile_lookup_res_add_relu_kernel(tc, tab, base, w, b, offs, out):
         codebook = held.tile([P, S], F32, name="codebook")
         base_sb = held.tile([P, N], F32, name="base_sb")
         weights = held.tile([P, M], BF16, name="weights")
-        biases = [held.tile([P, 1], F32, name=f"bias{c}") for c in range(M // P)]
+        bias = held.tile([P, 2], F32, name="bias")
 
         nc.sync.dma_start(offsets[:], offs)
         nc.sync.dma_start(codebook[:], tab[0])
         nc.scalar.dma_start(base_sb[:], base)
         nc.scalar.dma_start(weights[:], w)
-        for c in range(M // P):
-            nc.sync.dma_start(biases[c][:], b[c * P : (c + 1) * P, :])
+        nc.sync.dma_start(bias[:], b.rearrange("(p two) one -> p (two one)", two=2))
+        out_pairs = out.rearrange("(p two) n -> p two n", two=2)
 
         zeros = held.tile([P, 1], F32, name="zeros")
         nc.vector.memset(zeros[:], 0.0)
@@ -42,15 +42,15 @@ def tile_lookup_res_add_relu_kernel(tc, tab, base, w, b, offs, out):
             x_bf.append(held.tile([P, HALF], BF16, name=f"x_bf{h}"))
             nc.vector.tensor_copy(x_bf[h][:], x[:])
 
-        out0 = held.tile([P, N], F32, name="out0")
-        out1 = held.tile([P, N], F32, name="out1")
+        out_even = held.tile([P, N], F32, name="out_even")
+        out_odd = held.tile([P, N], F32, name="out_odd")
         for h in range(2):
             columns = slice(h * HALF, (h + 1) * HALF)
-            y0 = psum.tile([P, HALF], F32, name=f"y0_{h}")
-            nc.tensor.matmul(y0[:], weights[:, 0:P], x_bf[h][:], start=True, stop=True)
-            y1 = psum.tile([P, HALF], F32, name=f"y1_{h}")
-            nc.tensor.matmul(y1[:], weights[:, P : 2 * P], x_bf[h][:], start=True, stop=True)
-            nc.scalar.activation(out0[:, columns], y0[:], RELU, bias=biases[0][:])
-            nc.vector.tensor_scalar(out1[:, columns], y1[:], biases[1][:], 0.0, ADD, MAX)
-            nc.scalar.dma_start(out[0:P, columns], out0[:, columns])
-            nc.sync.dma_start(out[P : 2 * P, columns], out1[:, columns])
+            even = psum.tile([P, HALF], F32, name=f"even_{h}")
+            nc.tensor.matmul(even[:], weights[:, 0:M:2], x_bf[h][:], start=True, stop=True)
+            odd = psum.tile([P, HALF], F32, name=f"odd_{h}")
+            nc.tensor.matmul(odd[:], weights[:, 1:M:2], x_bf[h][:], start=True, stop=True)
+            nc.scalar.activation(out_even[:, columns], even[:], RELU, bias=bias[:, 0:1])
+            nc.vector.tensor_scalar(out_odd[:, columns], odd[:], bias[:, 1:2], 0.0, ADD, MAX)
+            nc.scalar.dma_start(out_pairs[:, 0, columns], out_even[:, columns])
+            nc.sync.dma_start(out_pairs[:, 1, columns], out_odd[:, columns])

import concourse.mybir as mybir

K, S, N, M = 128, 256, 256, 256
P = 128
HALF = N // 2
FLOPS = 2 * K * M * N + K * N
F32, BF16, U16 = mybir.dt.float32, mybir.dt.bfloat16, mybir.dt.uint16
ADD, MAX = mybir.AluOpType.add, mybir.AluOpType.max
RELU = mybir.ActivationFunctionType.Relu


def tile_lookup_res_add_relu_kernel(tc, tab, base, w, b, offs, out):
    nc = tc.nc
    with (
        tc.tile_pool(name="held", bufs=1) as held,
        tc.psum_pool(name="psum", bufs=1) as psum,
    ):
        offsets = held.tile([P, N // 16], U16, name="offsets")
        codebook = held.tile([P, S], F32, name="codebook")
        base_sb = held.tile([P, N], F32, name="base_sb")
        weights = held.tile([P, M], BF16, name="weights")
        bias = held.tile([P, 2], F32, name="bias")

        nc.sync.dma_start(offsets[:], offs)
        nc.sync.dma_start(codebook[:], tab[0])
        nc.scalar.dma_start(base_sb[:], base)
        nc.scalar.dma_start(weights[:], w)
        nc.sync.dma_start(bias[:], b.rearrange("(p two) one -> p (two one)", two=2))
        out_pairs = out.rearrange("(p two) n -> p two n", two=2)

        zeros = held.tile([P, 1], F32, name="zeros")
        nc.vector.memset(zeros[:], 0.0)
        warm = held.tile([P, 1], F32, name="warm")
        nc.scalar.activation(warm[:], zeros[:], RELU)

        x_bf = []
        for h in range(2):
            columns = slice(h * HALF, (h + 1) * HALF)
            entries = offsets[:, h * HALF // 16 : (h + 1) * HALF // 16]
            x = held.tile([P, HALF], F32, name=f"x{h}")
            nc.vector.tensor_tensor(x[:], codebook[:].indirect(entries), base_sb[:, columns], ADD)
            x_bf.append(held.tile([P, HALF], BF16, name=f"x_bf{h}"))
            nc.vector.tensor_copy(x_bf[h][:], x[:])

        out_even = held.tile([P, N], F32, name="out_even")
        out_odd = held.tile([P, N], F32, name="out_odd")
        for h in range(2):
            columns = slice(h * HALF, (h + 1) * HALF)
            even = psum.tile([P, HALF], F32, name=f"even_{h}")
            nc.tensor.matmul(even[:], weights[:, 0:M:2], x_bf[h][:], start=True, stop=True)
            odd = psum.tile([P, HALF], F32, name=f"odd_{h}")
            nc.tensor.matmul(odd[:], weights[:, 1:M:2], x_bf[h][:], start=True, stop=True)
            nc.scalar.activation(out_even[:, columns], even[:], RELU, bias=bias[:, 0:1])
            nc.vector.tensor_scalar(out_odd[:, columns], odd[:], bias[:, 1:2], 0.0, ADD, MAX)
            nc.scalar.dma_start(out_pairs[:, 0, columns], out_even[:, columns])
            nc.sync.dma_start(out_pairs[:, 1, columns], out_odd[:, columns])
